import numpy as np
import ml_dtypes


def mxq(x, axis, fmt="e4m3"):
    dtype, down = {"e4m3": (ml_dtypes.float8_e4m3fn, 7), "e5m2": (ml_dtypes.float8_e5m2, 14)}[fmt]
    v = np.moveaxis(np.asarray(x, np.float32).astype(ml_dtypes.bfloat16).astype(np.float64), axis, -1)
    blocks = v.reshape(v.shape[:-1] + (-1, 32))
    amax = np.abs(blocks).max(-1, keepdims=True)
    byte = np.maximum(np.where(amax > 0, np.frexp(amax)[1] - 1 + 127, 0) - down, 1)
    scale = np.exp2(byte - 127.0)
    codes = (blocks / scale).astype(np.float32).astype(dtype).astype(np.float64)
    return np.moveaxis((codes * scale).reshape(v.shape), -1, axis)


WIDE = False


def mx_kscale(k):
    if not WIDE:
        return np.ones(k)
    levels = np.array([10, -10, 5, -5, 0])
    if k % 512:
        return np.exp2(np.random.permutation(np.resize(levels, k // 32))).repeat(32)
    a = np.empty((k // 512, 16))
    for p in range(k // 512):
        a[p, :8] = np.random.permutation(np.resize(levels, 8))
        for g in range(8):
            far = levels[np.abs(levels - a[p, g]) >= 10]
            a[p, g + 8] = far[np.random.randint(len(far))]
    return np.exp2(a.ravel()).repeat(32)


def f64(x):
    return np.asarray(x).astype(np.float64)


def striped(idx):
    return np.tile(idx.reshape(-1, 16).T, (8, 1)).astype(np.uint16)


def unstriped(offs):
    return offs[:16].T.reshape(-1).astype(np.int64)


def pack_weight(w):
    k, n = w.shape
    w = f64(np.asarray(w, np.float32).astype(ml_dtypes.bfloat16)).reshape(k // 32, 32, n)
    amax = np.abs(w).max(1)
    byte = np.clip(np.where(amax > 0, np.frexp(amax)[1] - 1 + 127 - 7, 1), 1, 254)
    scaled = (w * np.exp2(127.0 - byte)[:, None, :]).reshape(k, n).astype(np.float32)
    words = np.ascontiguousarray(scaled.reshape(k // 512, 128, 4, n).transpose(0, 1, 3, 2)).astype(ml_dtypes.float8_e4m3fn).view(np.uint8)
    return words, np.ascontiguousarray(byte.astype(np.uint8).reshape(k // 512, 16, n))


def unpack_weight(words, scales):
    g, p, n, _ = words.shape
    vals = np.ascontiguousarray(words).view(ml_dtypes.float8_e4m3fn).astype(np.float64) * np.repeat(np.exp2(scales.astype(np.float64) - 127.0), 8, axis=1)[..., None]
    return vals.transpose(0, 1, 3, 2).reshape(g * 512, n)


K, T, S, V, N, D = 512, 1024, 512, 256, 128, 3
P = 2 ** 7


def setup_inputs():
    n = np.random.standard_normal
    s = mx_kscale(K)[:, None]
    near = np.random.permutation(S)
    packed_xT = pack_weight(n((K, T)) * s)
    return {
        "x_words": packed_xT[0],
        "x_scales": packed_xT[1],
        "w1": (n((K, N)) / np.sqrt(K) / s).astype(np.float32),
        "mixw": (np.tile(np.random.uniform(0.2, 1.0, (D, 1, V)), (1, P, 1))).astype(np.float32),
        "offs": striped(np.random.permutation(T)[:S]),
        "pos1": striped(near[:V]),
        "pos2": striped(near[V:]),
        "pos3": striped(np.random.permutation(S)[:V]),
        "right1": striped(np.random.permutation(S)[:V]),
        "right2": striped(np.random.permutation(S)[:V]),
        "right3": striped(np.random.permutation(S)[:V]),
    }


def reference(x_words, x_scales, w1, mixw, offs, pos1, pos2, pos3, right1, right2, right3):
    xq = unpack_weight(x_words, x_scales)[:, unstriped(offs)]
    h = mxq(f64(w1), 0, "e4m3").T @ xq
    g0 = h[:, unstriped(pos1)]
    g1 = h[:, unstriped(pos2)]
    g2 = h[:, unstriped(pos3)]
    return np.log((np.exp(g0 + h[:, unstriped(right1)])) * f64(mixw)[0, :1] + (np.exp(g1 + h[:, unstriped(right2)])) * f64(mixw)[1, :1] + (np.exp(g2 + h[:, unstriped(right3)])) * f64(mixw)[2, :1])

@@ -1,0 +1,140 @@
+from contextlib import ExitStack
+
+import concourse.mybir as mybir
+
+K, T, S, V, M, D = 512, 1024, 512, 256, 128, 3
+FLOPS = 2 * K * M * S
+
+F32 = mybir.dt.float32
+BF16 = mybir.dt.bfloat16
+I32 = mybir.dt.int32
+U32 = mybir.dt.uint32
+U16 = mybir.dt.uint16
+U8 = mybir.dt.uint8
+FP8X4 = mybir.dt.float8_e4m3fn_x4
+ALU = mybir.AluOpType
+ACT = mybir.ActivationFunctionType
+
+P = 128
+PACK = 4
+LIST_ROWS = 16
+PIECES = (256, 128, 128)
+
+
+def tile_picked_yspn_sum_p_kernel(
+    tc, x_words, x_scales, w1, mixw, offs, pos1, pos2, pos3, right1, right2, right3, out
+):
+    nc = tc.nc
+    with ExitStack() as ctx:
+        held = ctx.enter_context(tc.tile_pool(name="held", bufs=1))
+        psum = ctx.enter_context(tc.psum_pool(name="psum", bufs=1))
+
+        def load_list(name, src):
+            tile = held.tile(list(src.shape), U16, name=name)
+            nc.sync.dma_start(tile[:], src)
+            return tile
+
+        offs_t = load_list("offs_t", offs)
+
+        scale_table = held.tile([P, T], U8, align_bytes=64)
+        for q in range(4):
+            rows = x_scales[0][4 * q : 4 * q + 4, :].bitcast(I32)
+            nc.scalar.dma_start(
+                scale_table[32 * q : 32 * q + 32, :].bitcast(I32),
+                rows.unsqueeze(0).to_broadcast([8, 4, T // 4]),
+            )
+
+        w_raw = held.tile([P, PACK, M], F32)
+        nc.sync.dma_start(w_raw[:], w1.rearrange("(p j) m -> p j m", j=PACK))
+
+        word_table = held.tile([P, T], I32, align_bytes=64)
+        nc.sync.dma_start(word_table[:], x_words[0].rearrange("p n t -> p (n t)").bitcast(I32))
+
+        p0 = load_list("p0", pos1)
+        q0 = load_list("q0", right1)
+        p1 = load_list("p1", pos2)
+        q1 = load_list("q1", right2)
+        p2 = load_list("p2", pos3)
+        q2 = load_list("q2", right3)
+
+        mix = held.tile([P, D, V], F32)
+        nc.sync.dma_start(mix[:], mixw.rearrange("d p v -> p d v"))
+
+        w_grouped = held.tile([P, M, PACK], BF16, align_bytes=64)
+        nc.scalar.copy(w_grouped[:], w_raw[:].rearrange("p j m -> p m j"))
+        w_codes = held.tile([P, M], U32, align_bytes=64)
+        w_scales = held.tile([P, M], U8, align_bytes=64)
+
+        x_scale = held.tile([P, S], U8, align_bytes=64)
+        nc.vector.tensor_copy(x_scale[:], scale_table[:].indirect(offs_t[:]))
+
+        h = held.tile([P, S], F32, align_bytes=64)
+        start = 0
+        for i, n in enumerate(PIECES):
+            cols = slice(start, start + n)
+            x_codes = held.tile([P, n], I32, align_bytes=64, name="x_codes%d" % i)
+            nc.vector.tensor_copy(
+                x_codes[:].bitcast(U32),
+                word_table[:].bitcast(U32).indirect(offs_t[:, start // LIST_ROWS : (start + n) // LIST_ROWS]),
+            )
+            if i == 0:
+                nc.vector.quantize_mx(
+                    out=w_codes[:].bitcast(FP8X4),
+                    scales=w_scales[:],
+                    in_=w_grouped[:].rearrange("p m j -> p (m j)"),
+                )
+            acc = psum.tile([P, n], F32, name="acc%d" % i)
+            nc.tensor.matmul_mx(
+                out=acc[:],
+                lhsT=w_codes[:].bitcast(FP8X4),
+                lhsT_scale=w_scales[:],
+                rhs=x_codes[:].bitcast(FP8X4),
+                rhs_scale=x_scale[:, cols],
+                start=True,
+                stop=True,
+            )
+            if i == len(PIECES) - 1:
+                nc.vector.tensor_copy(h[:, cols], acc[:])
+            else:
+                nc.scalar.copy(h[:, cols], acc[:])
+            start = start + n
+
+        def work(name):
+            return held.tile([P, V], F32, align_bytes=64, name=name)
+
+        left0, a0, left1, u, top01, left2, d = (work(n) for n in ("left0", "a0", "left1", "u", "top01", "left2", "d"))
+        e01 = held.tile([P, 2, V], F32, align_bytes=64)
+        t01 = held.tile([P, 2, V], F32, align_bytes=64)
+        ea, eb, s01, ta, tb, total, top, logs, result = (
+            work(n) for n in ("ea", "eb", "s01", "ta", "tb", "total", "top", "logs", "result")
+        )
+        width = V // 2
+        parts = [(slice(c, c + width), slice(c // LIST_ROWS, (c + width) // LIST_ROWS)) for c in range(0, V, width)]
+
+        for c, o in parts:
+            nc.vector.tensor_copy(left0[:, c], h[:].indirect(p0[:, o]))
+        for c, o in parts:
+            nc.vector.tensor_tensor(a0[:, c], h[:].indirect(q0[:, o]), left0[:, c], ALU.add)
+        for c, o in parts:
+            nc.vector.tensor_tensor(left1[:, c], h[:].indirect(p1[:, o]), a0[:, c], ALU.subtract)
+        for c, o in parts:
+            nc.vector.tensor_tensor(u[:, c], h[:].indirect(q1[:, o]), left1[:, c], ALU.add)
+        for c, o in parts:
+            nc.vector.scalar_tensor_tensor(top01[:, c], u[:, c], 0.0, a0[:, c], ALU.max, ALU.add)
+        nc.scalar.activation(e01[:, 0, :], u[:], ACT.Exp, scale=-1.0)
+        nc.scalar.activation(e01[:, 1, :], u[:], ACT.Exp)
+        for c, o in parts:
+            nc.vector.tensor_tensor(left2[:, c], h[:].indirect(p2[:, o]), top01[:, c], ALU.subtract)
+        for c, o in parts:
+            nc.vector.tensor_tensor(d[:, c], h[:].indirect(q2[:, o]), left2[:, c], ALU.add)
+            nc.scalar.activation(eb[:, c], d[:, c], ACT.Exp)
+            nc.scalar.activation(ea[:, c], d[:, c], ACT.Exp, scale=-1.0)
+        nc.vector.scalar_tensor_tensor(t01[:], e01[:], 1.0, mix[:, 0:2, :], ALU.min, ALU.mult)
+        nc.vector.scalar_tensor_tensor(top[:], d[:], 0.0, top01[:], ALU.max, ALU.add)
+        nc.vector.tensor_tensor(s01[:], t01[:, 0, :], t01[:, 1, :], ALU.add)
+        nc.vector.scalar_tensor_tensor(tb[:], eb[:], 1.0, mix[:, 2, :], ALU.min, ALU.mult)
+        nc.vector.scalar_tensor_tensor(ta[:], ea[:], 1.0, s01[:], ALU.min, ALU.mult)
+        nc.vector.tensor_tensor(total[:], ta[:], tb[:], ALU.add)
+        nc.scalar.activation(logs[:], total[:], ACT.Ln)
+        nc.vector.tensor_tensor(result[:], logs[:], top[:], ALU.add)
+        nc.sync.dma_start(out, result[:])

@@ -39,7 +39,7 @@ def tile_picked_yspn_sum_p_kernel(
         scale_table = held.tile([P, T], U8, align_bytes=64)
         for q in range(4):
             rows = x_scales[0][4 * q : 4 * q + 4, :].bitcast(I32)
-            nc.scalar.dma_start(
+            (nc.sync if q < 2 else nc.scalar).dma_start(
                 scale_table[32 * q : 32 * q + 32, :].bitcast(I32),
                 rows.unsqueeze(0).to_broadcast([8, 4, T // 4]),
             )
@@ -60,7 +60,7 @@ def tile_picked_yspn_sum_p_kernel(
         mix = held.tile([P, D, V], F32)
         nc.sync.dma_start(mix[:], mixw.rearrange("d p v -> p d v"))
 
-        w_grouped = held.tile([P, M, PACK], BF16, align_bytes=64)
+        w_grouped = held.tile([P, M, PACK], BF16, align_bytes=64, tag="stage")
         nc.scalar.copy(w_grouped[:], w_raw[:].rearrange("p j m -> p m j"))
         w_codes = held.tile([P, M], U32, align_bytes=64)
         w_scales = held.tile([P, M], U8, align_bytes=64)
@@ -68,21 +68,21 @@ def tile_picked_yspn_sum_p_kernel(
         x_scale = held.tile([P, S], U8, align_bytes=64)
         nc.vector.tensor_copy(x_scale[:], scale_table[:].indirect(offs_t[:]))
 
+        nc.vector.quantize_mx(
+            out=w_codes[:].bitcast(FP8X4),
+            scales=w_scales[:],
+            in_=w_grouped[:].rearrange("p m j -> p (m j)"),
+        )
+
         h = held.tile([P, S], F32, align_bytes=64)
         start = 0
         for i, n in enumerate(PIECES):
             cols = slice(start, start + n)
-            x_codes = held.tile([P, n], I32, align_bytes=64, name="x_codes%d" % i)
+            x_codes = held.tile([P, n], I32, align_bytes=64, name="x_codes%d" % i, tag="stage" if i == 0 else "x_codes%d" % i)
             nc.vector.tensor_copy(
                 x_codes[:].bitcast(U32),
                 word_table[:].bitcast(U32).indirect(offs_t[:, start // LIST_ROWS : (start + n) // LIST_ROWS]),
             )
-            if i == 0:
-                nc.vector.quantize_mx(
-                    out=w_codes[:].bitcast(FP8X4),
-                    scales=w_scales[:],
-                    in_=w_grouped[:].rearrange("p m j -> p (m j)"),
-                )
             acc = psum.tile([P, n], F32, name="acc%d" % i)
             nc.tensor.matmul_mx(
                 out=acc[:],
@@ -130,11 +130,16 @@ def tile_picked_yspn_sum_p_kernel(
             nc.scalar.activation(eb[:, c], d[:, c], ACT.Exp)
             nc.scalar.activation(ea[:, c], d[:, c], ACT.Exp, scale=-1.0)
         nc.vector.scalar_tensor_tensor(t01[:], e01[:], 1.0, mix[:, 0:2, :], ALU.min, ALU.mult)
-        nc.vector.scalar_tensor_tensor(top[:], d[:], 0.0, top01[:], ALU.max, ALU.add)
-        nc.vector.tensor_tensor(s01[:], t01[:, 0, :], t01[:, 1, :], ALU.add)
         nc.vector.scalar_tensor_tensor(tb[:], eb[:], 1.0, mix[:, 2, :], ALU.min, ALU.mult)
-        nc.vector.scalar_tensor_tensor(ta[:], ea[:], 1.0, s01[:], ALU.min, ALU.mult)
-        nc.vector.tensor_tensor(total[:], ta[:], tb[:], ALU.add)
-        nc.scalar.activation(logs[:], total[:], ACT.Ln)
-        nc.vector.tensor_tensor(result[:], logs[:], top[:], ALU.add)
-        nc.sync.dma_start(out, result[:])
+        for c, o in parts:
+            nc.vector.tensor_tensor(s01[:, c], t01[:, 0, c], t01[:, 1, c], ALU.add)
+        for c, o in parts:
+            nc.vector.scalar_tensor_tensor(ta[:, c], ea[:, c], 1.0, s01[:, c], ALU.min, ALU.mult)
+        for c, o in parts:
+            nc.vector.tensor_tensor(total[:, c], ta[:, c], tb[:, c], ALU.add)
+        nc.vector.scalar_tensor_tensor(top[:], d[:], 0.0, top01[:], ALU.max, ALU.add)
+        for c, o in parts:
+            nc.scalar.activation(logs[:, c], total[:, c], ACT.Ln)
+        for (c, o), queue in zip(parts, (nc.sync, nc.scalar)):
+            nc.vector.tensor_tensor(result[:, c], logs[:, c], top[:, c], ALU.add)
+            queue.dma_start(out[:, c], result[:, c])

@@ -44,7 +44,7 @@ def tile_picked_yspn_sum_p_kernel(
                 rows.unsqueeze(0).to_broadcast([8, 4, T // 4]),
             )
 
-        w_raw = held.tile([P, PACK, M], F32)
+        w_raw = held.tile([P, PACK, M], F32, align_bytes=64, tag="stage")
         nc.sync.dma_start(w_raw[:], w1.rearrange("(p j) m -> p j m", j=PACK))
 
         word_table = held.tile([P, T], I32, align_bytes=64)
@@ -60,7 +60,7 @@ def tile_picked_yspn_sum_p_kernel(
         mix = held.tile([P, D, V], F32)
         nc.sync.dma_start(mix[:], mixw.rearrange("d p v -> p d v"))
 
-        w_grouped = held.tile([P, M, PACK], BF16, align_bytes=64, tag="stage")
+        w_grouped = held.tile([P, M, PACK], BF16, align_bytes=64)
         nc.scalar.copy(w_grouped[:], w_raw[:].rearrange("p j m -> p m j"))
         w_codes = held.tile([P, M], U32, align_bytes=64)
         w_scales = held.tile([P, M], U8, align_bytes=64)
@@ -74,13 +74,13 @@ def tile_picked_yspn_sum_p_kernel(
             in_=w_grouped[:].rearrange("p m j -> p (m j)"),
         )
 
+        x_codes = held.tile([P, S], I32, align_bytes=64, tag="stage")
         h = held.tile([P, S], F32, align_bytes=64)
         start = 0
         for i, n in enumerate(PIECES):
             cols = slice(start, start + n)
-            x_codes = held.tile([P, n], I32, align_bytes=64, name="x_codes%d" % i, tag="stage" if i == 0 else "x_codes%d" % i)
             nc.vector.tensor_copy(
-                x_codes[:].bitcast(U32),
+                x_codes[:, cols].bitcast(U32),
                 word_table[:].bitcast(U32).indirect(offs_t[:, start // LIST_ROWS : (start + n) // LIST_ROWS]),
             )
             acc = psum.tile([P, n], F32, name="acc%d" % i)
@@ -88,7 +88,7 @@ def tile_picked_yspn_sum_p_kernel(
                 out=acc[:],
                 lhsT=w_codes[:].bitcast(FP8X4),
                 lhsT_scale=w_scales[:],
-                rhs=x_codes[:].bitcast(FP8X4),
+                rhs=x_codes[:, cols].bitcast(FP8X4),
                 rhs_scale=x_scale[:, cols],
                 start=True,
                 stop=True,

@@ -2,8 +2,8 @@ from contextlib import ExitStack
 
 import concourse.mybir as mybir
 
-K, T, S, V, M, D = 512, 1024, 512, 256, 128, 3
-FLOPS = 2 * K * M * S
+K, LEAVES, PICKED, NODES, ROWS, TERMS = 512, 1024, 512, 256, 128, 3
+FLOPS = 2 * K * ROWS * PICKED
 
 F32 = mybir.dt.float32
 BF16 = mybir.dt.bfloat16
@@ -17,8 +17,11 @@ ACT = mybir.ActivationFunctionType
 
 P = 128
 PACK = 4
+QUADRANT = 32
+SCALE_ROWS = 4
 LIST_ROWS = 16
 PIECES = (256, 128, 128)
+HALF = NODES // 2
 
 
 def tile_picked_yspn_sum_p_kernel(
@@ -34,21 +37,27 @@ def tile_picked_yspn_sum_p_kernel(
             nc.sync.dma_start(tile[:], src)
             return tile
 
-        offs_t = load_list("offs_t", offs)
+        def entries(tile, cols):
+            return tile[:, cols.start // LIST_ROWS : cols.stop // LIST_ROWS]
 
-        scale_table = held.tile([P, T], U8, align_bytes=64)
-        for q in range(4):
-            rows = x_scales[0][4 * q : 4 * q + 4, :].bitcast(I32)
-            (nc.sync if q < 2 else nc.scalar).dma_start(
-                scale_table[32 * q : 32 * q + 32, :].bitcast(I32),
-                rows.unsqueeze(0).to_broadcast([8, 4, T // 4]),
+        def node_tile(name):
+            return held.tile([P, NODES], F32, align_bytes=64, name=name)
+
+        idx = load_list("idx", offs)
+
+        scale_table = held.tile([P, LEAVES], U8, align_bytes=64)
+        for quad, queue in enumerate((nc.sync, nc.sync, nc.scalar, nc.scalar)):
+            rows = x_scales[0][SCALE_ROWS * quad : SCALE_ROWS * (quad + 1), :].bitcast(I32)
+            queue.dma_start(
+                scale_table[QUADRANT * quad : QUADRANT * (quad + 1), :].bitcast(I32),
+                rows.unsqueeze(0).to_broadcast([QUADRANT // SCALE_ROWS, SCALE_ROWS, rows.shape[1]]),
             )
 
-        w_raw = held.tile([P, PACK, M], F32, align_bytes=64, tag="stage")
-        nc.sync.dma_start(w_raw[:], w1.rearrange("(p j) m -> p j m", j=PACK))
-
-        word_table = held.tile([P, T], I32, align_bytes=64)
+        word_table = held.tile([P, LEAVES], I32, align_bytes=64)
         nc.sync.dma_start(word_table[:], x_words[0].rearrange("p n t -> p (n t)").bitcast(I32))
+
+        w_raw = held.tile([P, PACK, ROWS], F32, align_bytes=64)
+        nc.sync.dma_start(w_raw[:], w1.rearrange("(p t) m -> p t m", t=PACK))
 
         p0 = load_list("p0", pos1)
         q0 = load_list("q0", right1)
@@ -57,89 +66,89 @@ def tile_picked_yspn_sum_p_kernel(
         p2 = load_list("p2", pos3)
         q2 = load_list("q2", right3)
 
-        mix = held.tile([P, D, V], F32)
+        mix = held.tile([P, TERMS, NODES], F32)
         nc.sync.dma_start(mix[:], mixw.rearrange("d p v -> p d v"))
 
-        w_grouped = held.tile([P, M, PACK], BF16, align_bytes=64)
-        nc.scalar.copy(w_grouped[:], w_raw[:].rearrange("p j m -> p m j"))
-        w_codes = held.tile([P, M], U32, align_bytes=64)
-        w_scales = held.tile([P, M], U8, align_bytes=64)
+        w_grouped = held.tile([P, ROWS, PACK], BF16, align_bytes=64)
+        nc.scalar.copy(w_grouped[:], w_raw[:].rearrange("p t m -> p m t"))
+        w_codes = held.tile([P, ROWS], U32, align_bytes=64)
+        w_scales = held.tile([P, ROWS], U8, align_bytes=64)
 
-        x_scale = held.tile([P, S], U8, align_bytes=64)
-        nc.vector.tensor_copy(x_scale[:], scale_table[:].indirect(offs_t[:]))
+        picked_scales = held.tile([P, PICKED], U8, align_bytes=64)
+        nc.vector.tensor_copy(picked_scales[:], scale_table[:].indirect(idx[:]))
 
         nc.vector.quantize_mx(
             out=w_codes[:].bitcast(FP8X4),
             scales=w_scales[:],
-            in_=w_grouped[:].rearrange("p m j -> p (m j)"),
+            in_=w_grouped[:].rearrange("p m t -> p (m t)"),
         )
 
-        x_codes = held.tile([P, S], I32, align_bytes=64, tag="stage")
-        h = held.tile([P, S], F32, align_bytes=64)
+        picked_words = held.tile([P, PICKED], I32, align_bytes=64)
+        h = held.tile([P, PICKED], F32, align_bytes=64)
         start = 0
-        for i, n in enumerate(PIECES):
-            cols = slice(start, start + n)
+        for piece, width in enumerate(PIECES):
+            cols = slice(start, start + width)
             nc.vector.tensor_copy(
-                x_codes[:, cols].bitcast(U32),
-                word_table[:].bitcast(U32).indirect(offs_t[:, start // LIST_ROWS : (start + n) // LIST_ROWS]),
+                picked_words[:, cols].bitcast(U32),
+                word_table[:].bitcast(U32).indirect(entries(idx, cols)),
             )
-            acc = psum.tile([P, n], F32, name="acc%d" % i)
+            acc = psum.tile([P, width], F32, name="acc%d" % piece)
             nc.tensor.matmul_mx(
                 out=acc[:],
                 lhsT=w_codes[:].bitcast(FP8X4),
                 lhsT_scale=w_scales[:],
-                rhs=x_codes[:, cols].bitcast(FP8X4),
-                rhs_scale=x_scale[:, cols],
+                rhs=picked_words[:, cols].bitcast(FP8X4),
+                rhs_scale=picked_scales[:, cols],
                 start=True,
                 stop=True,
             )
-            if i == len(PIECES) - 1:
+            if piece == len(PIECES) - 1:
                 nc.vector.tensor_copy(h[:, cols], acc[:])
             else:
                 nc.scalar.copy(h[:, cols], acc[:])
-            start = start + n
+            start = start + width
 
-        def work(name):
-            return held.tile([P, V], F32, align_bytes=64, name=name)
-
-        left0, a0, left1, u, top01, left2, d = (work(n) for n in ("left0", "a0", "left1", "u", "top01", "left2", "d"))
-        e01 = held.tile([P, 2, V], F32, align_bytes=64)
-        t01 = held.tile([P, 2, V], F32, align_bytes=64)
-        ea, eb, s01, ta, tb, total, top, logs, result = (
-            work(n) for n in ("ea", "eb", "s01", "ta", "tb", "total", "top", "logs", "result")
+        left0, a0, left1, gap01, top01, left2, gap2 = (
+            node_tile(name) for name in ("left0", "a0", "left1", "gap01", "top01", "left2", "gap2")
         )
-        width = V // 2
-        parts = [(slice(c, c + width), slice(c // LIST_ROWS, (c + width) // LIST_ROWS)) for c in range(0, V, width)]
+        exp01 = held.tile([P, 2, NODES], F32, align_bytes=64)
+        term01 = held.tile([P, 2, NODES], F32, align_bytes=64)
+        exp_down, exp_up, sum01, kept01, term2, total, top, logs, result = (
+            node_tile(name)
+            for name in ("exp_down", "exp_up", "sum01", "kept01", "term2", "total", "top", "logs", "result")
+        )
+        halves = [slice(c, c + HALF) for c in range(0, NODES, HALF)]
 
-        for c, o in parts:
-            nc.vector.tensor_copy(left0[:, c], h[:].indirect(p0[:, o]))
-        for c, o in parts:
-            nc.vector.tensor_tensor(a0[:, c], h[:].indirect(q0[:, o]), left0[:, c], ALU.add)
-        for c, o in parts:
-            nc.vector.tensor_tensor(left1[:, c], h[:].indirect(p1[:, o]), a0[:, c], ALU.subtract)
-        for c, o in parts:
-            nc.vector.tensor_tensor(u[:, c], h[:].indirect(q1[:, o]), left1[:, c], ALU.add)
-        for c, o in parts:
-            nc.vector.scalar_tensor_tensor(top01[:, c], u[:, c], 0.0, a0[:, c], ALU.max, ALU.add)
-        nc.scalar.activation(e01[:, 0, :], u[:], ACT.Exp, scale=-1.0)
-        nc.scalar.activation(e01[:, 1, :], u[:], ACT.Exp)
-        for c, o in parts:
-            nc.vector.tensor_tensor(left2[:, c], h[:].indirect(p2[:, o]), top01[:, c], ALU.subtract)
-        for c, o in parts:
-            nc.vector.tensor_tensor(d[:, c], h[:].indirect(q2[:, o]), left2[:, c], ALU.add)
-            nc.scalar.activation(eb[:, c], d[:, c], ACT.Exp)
-            nc.scalar.activation(ea[:, c], d[:, c], ACT.Exp, scale=-1.0)
-        nc.vector.scalar_tensor_tensor(t01[:], e01[:], 1.0, mix[:, 0:2, :], ALU.min, ALU.mult)
-        nc.vector.scalar_tensor_tensor(tb[:], eb[:], 1.0, mix[:, 2, :], ALU.min, ALU.mult)
-        for c, o in parts:
-            nc.vector.tensor_tensor(s01[:, c], t01[:, 0, c], t01[:, 1, c], ALU.add)
-        for c, o in parts:
-            nc.vector.scalar_tensor_tensor(ta[:, c], ea[:, c], 1.0, s01[:, c], ALU.min, ALU.mult)
-        for c, o in parts:
-            nc.vector.tensor_tensor(total[:, c], ta[:, c], tb[:, c], ALU.add)
-        nc.vector.scalar_tensor_tensor(top[:], d[:], 0.0, top01[:], ALU.max, ALU.add)
-        for c, o in parts:
+        def gather_and(dst, listed, other, op):
+            for c in halves:
+                nc.vector.tensor_tensor(dst[:, c], h[:].indirect(entries(listed, c)), other[:, c], op)
+
+        for c in halves:
+            nc.vector.tensor_copy(left0[:, c], h[:].indirect(entries(p0, c)))
+        gather_and(a0, q0, left0, ALU.add)
+        gather_and(left1, p1, a0, ALU.subtract)
+        gather_and(gap01, q1, left1, ALU.add)
+        for c in halves:
+            nc.vector.scalar_tensor_tensor(top01[:, c], gap01[:, c], 0.0, a0[:, c], ALU.max, ALU.add)
+        nc.scalar.activation(exp01[:, 0, :], gap01[:], ACT.Exp, scale=-1.0)
+        nc.scalar.activation(exp01[:, 1, :], gap01[:], ACT.Exp)
+        gather_and(left2, p2, top01, ALU.subtract)
+        for c in halves:
+            nc.vector.tensor_tensor(gap2[:, c], h[:].indirect(entries(q2, c)), left2[:, c], ALU.add)
+            nc.scalar.activation(exp_up[:, c], gap2[:, c], ACT.Exp)
+            nc.scalar.activation(exp_down[:, c], gap2[:, c], ACT.Exp, scale=-1.0)
+
+        nc.vector.scalar_tensor_tensor(term01[:], exp01[:], 1.0, mix[:, 0:2, :], ALU.min, ALU.mult)
+        nc.vector.scalar_tensor_tensor(term2[:], exp_up[:], 1.0, mix[:, 2, :], ALU.min, ALU.mult)
+        for c in halves:
+            nc.vector.tensor_tensor(sum01[:, c], term01[:, 0, c], term01[:, 1, c], ALU.add)
+        for c in halves:
+            nc.vector.scalar_tensor_tensor(kept01[:, c], exp_down[:, c], 1.0, sum01[:, c], ALU.min, ALU.mult)
+        for c in halves:
+            nc.vector.tensor_tensor(total[:, c], kept01[:, c], term2[:, c], ALU.add)
+        nc.vector.scalar_tensor_tensor(top[:], gap2[:], 0.0, top01[:], ALU.max, ALU.add)
+        for c in halves:
             nc.scalar.activation(logs[:, c], total[:, c], ACT.Ln)
-        for (c, o), queue in zip(parts, (nc.sync, nc.scalar)):
+        for c, queue in zip(halves, (nc.sync, nc.scalar)):
             nc.vector.tensor_tensor(result[:, c], logs[:, c], top[:, c], ALU.add)
             queue.dma_start(out[:, c], result[:, c])

@@ -1,3 +1,4 @@
+import math
 from contextlib import ExitStack
 
 import concourse.mybir as mybir
@@ -22,6 +23,7 @@ SCALE_ROWS = 4
 LIST_ROWS = 16
 PIECES = (256, 128, 128)
 HALF = NODES // 2
+REACH = 32.0
 
 
 def tile_picked_yspn_sum_p_kernel(
@@ -70,7 +72,10 @@ def tile_picked_yspn_sum_p_kernel(
         nc.sync.dma_start(mix[:], mixw.rearrange("d p v -> p d v"))
 
         w_grouped = held.tile([P, ROWS, PACK], BF16, align_bytes=64)
-        nc.scalar.copy(w_grouped[:], w_raw[:].rearrange("p t m -> p m t"))
+        nc.scalar.copy(
+            w_grouped[:].rearrange("p (c i) t -> p c t i", i=PACK),
+            w_raw[:].rearrange("p t (c i) -> p c t i", i=PACK),
+        )
         w_codes = held.tile([P, ROWS], U32, align_bytes=64)
         w_scales = held.tile([P, ROWS], U8, align_bytes=64)
 
@@ -84,14 +89,11 @@ def tile_picked_yspn_sum_p_kernel(
         )
 
         picked_words = held.tile([P, PICKED], I32, align_bytes=64)
+        nc.vector.tensor_copy(picked_words[:].bitcast(U32), word_table[:].bitcast(U32).indirect(idx[:]))
         h = held.tile([P, PICKED], F32, align_bytes=64)
         start = 0
         for piece, width in enumerate(PIECES):
             cols = slice(start, start + width)
-            nc.vector.tensor_copy(
-                picked_words[:, cols].bitcast(U32),
-                word_table[:].bitcast(U32).indirect(entries(idx, cols)),
-            )
             acc = psum.tile([P, width], F32, name="acc%d" % piece)
             nc.tensor.matmul_mx(
                 out=acc[:],
@@ -113,9 +115,8 @@ def tile_picked_yspn_sum_p_kernel(
         )
         exp01 = held.tile([P, 2, NODES], F32, align_bytes=64)
         term01 = held.tile([P, 2, NODES], F32, align_bytes=64)
-        exp_down, exp_up, sum01, kept01, term2, total, top, logs, result = (
-            node_tile(name)
-            for name in ("exp_down", "exp_up", "sum01", "kept01", "term2", "total", "top", "logs", "result")
+        exp_up, sum01, term2, total, top, logs, result = (
+            node_tile(name) for name in ("exp_up", "sum01", "term2", "total", "top", "logs", "result")
         )
         halves = [slice(c, c + HALF) for c in range(0, NODES, HALF)]
 
@@ -133,22 +134,18 @@ def tile_picked_yspn_sum_p_kernel(
         nc.scalar.activation(exp01[:, 0, :], gap01[:], ACT.Exp, scale=-1.0)
         nc.scalar.activation(exp01[:, 1, :], gap01[:], ACT.Exp)
         gather_and(left2, p2, top01, ALU.subtract)
-        for c in halves:
+        for c in (slice(0, 128), slice(128, 192), slice(192, 256)):
             nc.vector.tensor_tensor(gap2[:, c], h[:].indirect(entries(q2, c)), left2[:, c], ALU.add)
             nc.scalar.activation(exp_up[:, c], gap2[:, c], ACT.Exp)
-            nc.scalar.activation(exp_down[:, c], gap2[:, c], ACT.Exp, scale=-1.0)
 
-        nc.vector.scalar_tensor_tensor(term01[:], exp01[:], 1.0, mix[:, 0:2, :], ALU.min, ALU.mult)
-        nc.vector.scalar_tensor_tensor(term2[:], exp_up[:], 1.0, mix[:, 2, :], ALU.min, ALU.mult)
-        for c in halves:
-            nc.vector.tensor_tensor(sum01[:, c], term01[:, 0, c], term01[:, 1, c], ALU.add)
-        for c in halves:
-            nc.vector.scalar_tensor_tensor(kept01[:, c], exp_down[:, c], 1.0, sum01[:, c], ALU.min, ALU.mult)
-        for c in halves:
-            nc.vector.tensor_tensor(total[:, c], kept01[:, c], term2[:, c], ALU.add)
-        nc.vector.scalar_tensor_tensor(top[:], gap2[:], 0.0, top01[:], ALU.max, ALU.add)
+        nc.vector.scalar_tensor_tensor(term01[:, 0, :], exp01[:, 0, :], 1.0, mix[:, 0, :], ALU.min, ALU.mult)
+        nc.vector.scalar_tensor_tensor(term01[:, 1, :], exp01[:, 1, :], 1.0, mix[:, 1, :], ALU.min, ALU.mult)
+        nc.vector.scalar_tensor_tensor(term2[:], exp_up[:], math.exp(REACH), mix[:, 2, :], ALU.min, ALU.mult)
+        nc.vector.tensor_tensor(sum01[:], term01[:, 0, :], term01[:, 1, :], ALU.add)
+        nc.vector.scalar_tensor_tensor(top[:], gap2[:], REACH, top01[:], ALU.max, ALU.add)
+        nc.vector.tensor_tensor(total[:], sum01[:], term2[:], ALU.add)
         for c in halves:
             nc.scalar.activation(logs[:, c], total[:, c], ACT.Ln)
         for c, queue in zip(halves, (nc.sync, nc.scalar)):
-            nc.vector.tensor_tensor(result[:, c], logs[:, c], top[:, c], ALU.add)
+            nc.vector.scalar_tensor_tensor(result[:, c], top[:, c], REACH, logs[:, c], ALU.subtract, ALU.add)
             queue.dma_start(out[:, c], result[:, c])

@@ -21,7 +21,7 @@ PACK = 4
 QUADRANT = 32
 SCALE_ROWS = 4
 LIST_ROWS = 16
-PIECES = (256, 128, 128)
+PIECES = (128, 128, 128, 128)
 HALF = NODES // 2
 REACH = 32.0
 
@@ -42,8 +42,8 @@ def tile_picked_yspn_sum_p_kernel(
         def entries(tile, cols):
             return tile[:, cols.start // LIST_ROWS : cols.stop // LIST_ROWS]
 
-        def node_tile(name):
-            return held.tile([P, NODES], F32, align_bytes=64, name=name)
+        def node_tile(name, tag=None):
+            return held.tile([P, NODES], F32, align_bytes=64, name=name, tag=tag or name)
 
         idx = load_list("idx", offs)
 
@@ -104,14 +104,14 @@ def tile_picked_yspn_sum_p_kernel(
                 start=True,
                 stop=True,
             )
-            if piece == len(PIECES) - 1:
+            if piece < 2:
                 nc.vector.tensor_copy(h[:, cols], acc[:])
             else:
                 nc.scalar.copy(h[:, cols], acc[:])
             start = start + width
 
-        left0, a0, left1, gap01, top01, left2, gap2 = (
-            node_tile(name) for name in ("left0", "a0", "left1", "gap01", "top01", "left2", "gap2")
+        left0, a0, left1, gap01, left2, short2, gap2 = (
+            node_tile(name) for name in ("left0", "a0", "left1", "gap01", "left2", "short2", "gap2")
         )
         exp01 = held.tile([P, 2, NODES], F32, align_bytes=64)
         term01 = held.tile([P, 2, NODES], F32, align_bytes=64)
@@ -128,16 +128,18 @@ def tile_picked_yspn_sum_p_kernel(
             nc.vector.tensor_copy(left0[:, c], h[:].indirect(entries(p0, c)))
         gather_and(a0, q0, left0, ALU.add)
         gather_and(left1, p1, a0, ALU.subtract)
+        nc.vector.tensor_tensor(left2[:], h[:].indirect(p2[:]), a0[:], ALU.subtract)
         gather_and(gap01, q1, left1, ALU.add)
         for c in halves:
-            nc.vector.scalar_tensor_tensor(top01[:, c], gap01[:, c], 0.0, a0[:, c], ALU.max, ALU.add)
+            nc.vector.scalar_tensor_tensor(short2[:, c], gap01[:, c], 0.0, left2[:, c], ALU.max, ALU.subtract)
         nc.scalar.activation(exp01[:, 0, :], gap01[:], ACT.Exp, scale=-1.0)
         nc.scalar.activation(exp01[:, 1, :], gap01[:], ACT.Exp)
-        gather_and(left2, p2, top01, ALU.subtract)
         for c in (slice(0, 128), slice(128, 192), slice(192, 256)):
-            nc.vector.tensor_tensor(gap2[:, c], h[:].indirect(entries(q2, c)), left2[:, c], ALU.add)
+            nc.vector.tensor_tensor(gap2[:, c], h[:].indirect(entries(q2, c)), short2[:, c], ALU.subtract)
             nc.scalar.activation(exp_up[:, c], gap2[:, c], ACT.Exp)
 
+        top01 = node_tile("top01", tag="short2")
+        nc.vector.scalar_tensor_tensor(top01[:], gap01[:], 0.0, a0[:], ALU.max, ALU.add)
         nc.vector.scalar_tensor_tensor(term01[:, 0, :], exp01[:, 0, :], 1.0, mix[:, 0, :], ALU.min, ALU.mult)
         nc.vector.scalar_tensor_tensor(term01[:, 1, :], exp01[:, 1, :], 1.0, mix[:, 1, :], ALU.min, ALU.mult)
         nc.vector.scalar_tensor_tensor(term2[:], exp_up[:], math.exp(REACH), mix[:, 2, :], ALU.min, ALU.mult)

@@ -18,12 +18,15 @@ ACT = mybir.ActivationFunctionType
 
 P = 128
 PACK = 4
+LINE = 4
 QUADRANT = 32
 SCALE_ROWS = 4
 LIST_ROWS = 16
-PIECES = (128, 128, 128, 128)
+PIECE = 128
+PIECES_ON_VECTOR = 2
 HALF = NODES // 2
-REACH = 32.0
+LAST_WIDTHS = (128, 64, 64)
+REACH = 40.0
 
 
 def tile_picked_yspn_sum_p_kernel(
@@ -42,8 +45,8 @@ def tile_picked_yspn_sum_p_kernel(
         def entries(tile, cols):
             return tile[:, cols.start // LIST_ROWS : cols.stop // LIST_ROWS]
 
-        def node_tile(name, tag=None):
-            return held.tile([P, NODES], F32, align_bytes=64, name=name, tag=tag or name)
+        def node_tile(name, bytes_of=None):
+            return held.tile([P, NODES], F32, align_bytes=64, name=name, tag=bytes_of or name)
 
         idx = load_list("idx", offs)
 
@@ -73,8 +76,8 @@ def tile_picked_yspn_sum_p_kernel(
 
         w_grouped = held.tile([P, ROWS, PACK], BF16, align_bytes=64)
         nc.scalar.copy(
-            w_grouped[:].rearrange("p (c i) t -> p c t i", i=PACK),
-            w_raw[:].rearrange("p t (c i) -> p c t i", i=PACK),
+            w_grouped[:].rearrange("p (c i) t -> p c t i", i=LINE),
+            w_raw[:].rearrange("p t (c i) -> p c t i", i=LINE),
         )
         w_codes = held.tile([P, ROWS], U32, align_bytes=64)
         w_scales = held.tile([P, ROWS], U8, align_bytes=64)
@@ -90,11 +93,11 @@ def tile_picked_yspn_sum_p_kernel(
 
         picked_words = held.tile([P, PICKED], I32, align_bytes=64)
         nc.vector.tensor_copy(picked_words[:].bitcast(U32), word_table[:].bitcast(U32).indirect(idx[:]))
+
         h = held.tile([P, PICKED], F32, align_bytes=64)
-        start = 0
-        for piece, width in enumerate(PIECES):
-            cols = slice(start, start + width)
-            acc = psum.tile([P, width], F32, name="acc%d" % piece)
+        for piece in range(PICKED // PIECE):
+            cols = slice(piece * PIECE, (piece + 1) * PIECE)
+            acc = psum.tile([P, PIECE], F32, name="acc%d" % piece)
             nc.tensor.matmul_mx(
                 out=acc[:],
                 lhsT=w_codes[:].bitcast(FP8X4),
@@ -104,19 +107,18 @@ def tile_picked_yspn_sum_p_kernel(
                 start=True,
                 stop=True,
             )
-            if piece < 2:
+            if piece < PIECES_ON_VECTOR:
                 nc.vector.tensor_copy(h[:, cols], acc[:])
             else:
                 nc.scalar.copy(h[:, cols], acc[:])
-            start = start + width
 
         left0, a0, left1, gap01, left2, short2, gap2 = (
             node_tile(name) for name in ("left0", "a0", "left1", "gap01", "left2", "short2", "gap2")
         )
         exp01 = held.tile([P, 2, NODES], F32, align_bytes=64)
         term01 = held.tile([P, 2, NODES], F32, align_bytes=64)
-        exp_up, sum01, term2, total, top, logs, result = (
-            node_tile(name) for name in ("exp_up", "sum01", "term2", "total", "top", "logs", "result")
+        exp2, sum01, term2, total, top, logs, result = (
+            node_tile(name) for name in ("exp2", "sum01", "term2", "total", "top", "logs", "result")
         )
         halves = [slice(c, c + HALF) for c in range(0, NODES, HALF)]
 
@@ -134,18 +136,20 @@ def tile_picked_yspn_sum_p_kernel(
             nc.vector.scalar_tensor_tensor(short2[:, c], gap01[:, c], 0.0, left2[:, c], ALU.max, ALU.subtract)
         nc.scalar.activation(exp01[:, 0, :], gap01[:], ACT.Exp, scale=-1.0)
         nc.scalar.activation(exp01[:, 1, :], gap01[:], ACT.Exp)
-        for c in (slice(0, 128), slice(128, 192), slice(192, 256)):
+        start = 0
+        for width in LAST_WIDTHS:
+            c = slice(start, start + width)
             nc.vector.tensor_tensor(gap2[:, c], h[:].indirect(entries(q2, c)), short2[:, c], ALU.subtract)
-            nc.scalar.activation(exp_up[:, c], gap2[:, c], ACT.Exp)
+            nc.scalar.activation(exp2[:, c], gap2[:, c], ACT.Exp)
+            start = start + width
 
-        top01 = node_tile("top01", tag="short2")
-        nc.vector.scalar_tensor_tensor(top01[:], gap01[:], 0.0, a0[:], ALU.max, ALU.add)
-        nc.vector.scalar_tensor_tensor(term01[:, 0, :], exp01[:, 0, :], 1.0, mix[:, 0, :], ALU.min, ALU.mult)
-        nc.vector.scalar_tensor_tensor(term01[:, 1, :], exp01[:, 1, :], 1.0, mix[:, 1, :], ALU.min, ALU.mult)
-        nc.vector.scalar_tensor_tensor(term2[:], exp_up[:], math.exp(REACH), mix[:, 2, :], ALU.min, ALU.mult)
+        nc.vector.scalar_tensor_tensor(term01[:], exp01[:], 1.0, mix[:, 0:2, :], ALU.min, ALU.mult)
+        nc.vector.scalar_tensor_tensor(term2[:], exp2[:], math.exp(REACH), mix[:, 2, :], ALU.min, ALU.mult)
         nc.vector.tensor_tensor(sum01[:], term01[:, 0, :], term01[:, 1, :], ALU.add)
-        nc.vector.scalar_tensor_tensor(top[:], gap2[:], REACH, top01[:], ALU.max, ALU.add)
+        top01 = node_tile("top01", bytes_of="exp2")
+        nc.vector.scalar_tensor_tensor(top01[:], gap01[:], 0.0, a0[:], ALU.max, ALU.add)
         nc.vector.tensor_tensor(total[:], sum01[:], term2[:], ALU.add)
+        nc.vector.scalar_tensor_tensor(top[:], gap2[:], REACH, top01[:], ALU.max, ALU.add)
         for c in halves:
             nc.scalar.activation(logs[:, c], total[:, c], ACT.Ln)
         for c, queue in zip(halves, (nc.sync, nc.scalar)):

@@ -126,22 +126,27 @@ def tile_picked_yspn_sum_p_kernel(
             for c in halves:
                 nc.vector.tensor_tensor(dst[:, c], h[:].indirect(entries(listed, c)), other[:, c], op)
 
+        first, second = halves
+
+        def gather_half(dst, listed, other, op, c):
+            nc.vector.tensor_tensor(dst[:, c], h[:].indirect(entries(listed, c)), other[:, c], op)
+
         for c in halves:
             nc.vector.tensor_copy(left0[:, c], h[:].indirect(entries(p0, c)))
         gather_and(a0, q0, left0, ALU.add)
         gather_and(left1, p1, a0, ALU.subtract)
         nc.vector.tensor_tensor(left2[:], h[:].indirect(p2[:]), a0[:], ALU.subtract)
-        gather_and(gap01, q1, left1, ALU.add)
+        gather_half(gap01, q1, left1, ALU.add, first)
+        gather_half(short2, q2, left2, ALU.add, second)
+        nc.vector.scalar_tensor_tensor(short2[:, first], gap01[:, first], 0.0, left2[:, first], ALU.max, ALU.subtract)
+        gather_half(gap01, q1, left1, ALU.add, second)
+        gather_half(gap2, q2, short2, ALU.subtract, first)
+        nc.vector.scalar_tensor_tensor(gap2[:, second], gap01[:, second], 0.0, short2[:, second], ALU.max, ALU.subtract)
         for c in halves:
-            nc.vector.scalar_tensor_tensor(short2[:, c], gap01[:, c], 0.0, left2[:, c], ALU.max, ALU.subtract)
-        nc.scalar.activation(exp01[:, 0, :], gap01[:], ACT.Exp, scale=-1.0)
-        nc.scalar.activation(exp01[:, 1, :], gap01[:], ACT.Exp)
-        start = 0
-        for width in LAST_WIDTHS:
-            c = slice(start, start + width)
-            nc.vector.tensor_tensor(gap2[:, c], h[:].indirect(entries(q2, c)), short2[:, c], ALU.subtract)
-            nc.scalar.activation(exp2[:, c], gap2[:, c], ACT.Exp)
-            start = start + width
+            nc.scalar.activation(exp01[:, 0, c], gap01[:, c], ACT.Exp, scale=-1.0)
+            nc.scalar.activation(exp01[:, 1, c], gap01[:, c], ACT.Exp)
+        nc.scalar.activation(exp2[:, first], gap2[:, first], ACT.Exp)
+        nc.scalar.activation(exp2[:, second], gap2[:, second], ACT.Exp, scale=-1.0)
 
         nc.vector.scalar_tensor_tensor(term01[:], exp01[:], 1.0, mix[:, 0:2, :], ALU.min, ALU.mult)
         nc.vector.scalar_tensor_tensor(term2[:], exp2[:], math.exp(REACH), mix[:, 2, :], ALU.min, ALU.mult)
@@ -149,9 +154,10 @@ def tile_picked_yspn_sum_p_kernel(
         top01 = node_tile("top01", bytes_of="exp2")
         nc.vector.scalar_tensor_tensor(top01[:], gap01[:], 0.0, a0[:], ALU.max, ALU.add)
         nc.vector.tensor_tensor(total[:], sum01[:], term2[:], ALU.add)
-        nc.vector.scalar_tensor_tensor(top[:], gap2[:], REACH, top01[:], ALU.max, ALU.add)
+        nc.vector.scalar_tensor_tensor(top[:, first], gap2[:, first], REACH, top01[:, first], ALU.max, ALU.add)
+        nc.vector.scalar_tensor_tensor(top[:, second], gap2[:, second], -REACH, top01[:, second], ALU.min, ALU.subtract)
         for c in halves:
             nc.scalar.activation(logs[:, c], total[:, c], ACT.Ln)
-        for c, queue in zip(halves, (nc.sync, nc.scalar)):
-            nc.vector.scalar_tensor_tensor(result[:, c], top[:, c], REACH, logs[:, c], ALU.subtract, ALU.add)
+        for c, queue, op in zip(halves, (nc.sync, nc.scalar), (ALU.add, ALU.subtract)):
+            nc.vector.scalar_tensor_tensor(result[:, c], logs[:, c], REACH, top[:, c], ALU.subtract, op)
             queue.dma_start(out[:, c], result[:, c])

@@ -116,7 +116,7 @@ def tile_picked_yspn_sum_p_kernel(
             node_tile(name) for name in ("left0", "a0", "left1", "gap01", "left2", "short2", "gap2")
         )
         exp01 = held.tile([P, 2, NODES], F32, align_bytes=64)
-        term01 = held.tile([P, 2, NODES], F32, align_bytes=64)
+        term01 = held.tile([P, 2, NODES], F32, align_bytes=64, tag="term01")
         exp2, sum01, term2, total, top, logs, result = (
             node_tile(name) for name in ("exp2", "sum01", "term2", "total", "top", "logs", "result")
         )
@@ -136,28 +136,31 @@ def tile_picked_yspn_sum_p_kernel(
         gather_and(a0, q0, left0, ALU.add)
         gather_and(left1, p1, a0, ALU.subtract)
         nc.vector.tensor_tensor(left2[:], h[:].indirect(p2[:]), a0[:], ALU.subtract)
+        gaps01 = (gap01[:, first], left1[:, first])
         gather_half(gap01, q1, left1, ALU.add, first)
         gather_half(short2, q2, left2, ALU.add, second)
-        nc.vector.scalar_tensor_tensor(short2[:, first], gap01[:, first], 0.0, left2[:, first], ALU.max, ALU.subtract)
-        gather_half(gap01, q1, left1, ALU.add, second)
+        nc.vector.scalar_tensor_tensor(short2[:, first], gaps01[0], 0.0, left2[:, first], ALU.max, ALU.subtract)
+        nc.vector.tensor_tensor(gaps01[1], h[:].indirect(entries(q1, second)), left1[:, second], ALU.add)
         gather_half(gap2, q2, short2, ALU.subtract, first)
-        nc.vector.scalar_tensor_tensor(gap2[:, second], gap01[:, second], 0.0, short2[:, second], ALU.max, ALU.subtract)
-        for c in halves:
-            nc.scalar.activation(exp01[:, 0, c], gap01[:, c], ACT.Exp, scale=-1.0)
-            nc.scalar.activation(exp01[:, 1, c], gap01[:, c], ACT.Exp)
+        nc.vector.scalar_tensor_tensor(gap2[:, second], gaps01[1], 0.0, short2[:, second], ALU.max, ALU.subtract)
+        for c, gap in zip(halves, gaps01):
+            nc.scalar.activation(exp01[:, 0, c], gap, ACT.Exp, scale=-1.0)
+            nc.scalar.activation(exp01[:, 1, c], gap, ACT.Exp)
         nc.scalar.activation(exp2[:, first], gap2[:, first], ACT.Exp)
         nc.scalar.activation(exp2[:, second], gap2[:, second], ACT.Exp, scale=-1.0)
 
-        nc.vector.scalar_tensor_tensor(term01[:], exp01[:], 1.0, mix[:, 0:2, :], ALU.min, ALU.mult)
+        for c in halves:
+            nc.vector.scalar_tensor_tensor(term01[:, :, c], exp01[:, :, c], 1.0, mix[:, 0:2, c], ALU.min, ALU.mult)
         nc.vector.scalar_tensor_tensor(term2[:], exp2[:], math.exp(REACH), mix[:, 2, :], ALU.min, ALU.mult)
         nc.vector.tensor_tensor(sum01[:], term01[:, 0, :], term01[:, 1, :], ALU.add)
-        top01 = node_tile("top01", bytes_of="exp2")
-        nc.vector.scalar_tensor_tensor(top01[:], gap01[:], 0.0, a0[:], ALU.max, ALU.add)
-        nc.vector.tensor_tensor(total[:], sum01[:], term2[:], ALU.add)
-        nc.vector.scalar_tensor_tensor(top[:, first], gap2[:, first], REACH, top01[:, first], ALU.max, ALU.add)
-        nc.vector.scalar_tensor_tensor(top[:, second], gap2[:, second], -REACH, top01[:, second], ALU.min, ALU.subtract)
+        nc.vector.scalar_tensor_tensor(exp2[:, first], gaps01[0], 0.0, a0[:, first], ALU.max, ALU.add)
+        nc.vector.scalar_tensor_tensor(exp2[:, second], gaps01[1], REACH, short2[:, second], ALU.add, ALU.max)
+        for c in halves:
+            nc.vector.tensor_tensor(total[:, c], sum01[:, c], term2[:, c], ALU.add)
+        nc.vector.scalar_tensor_tensor(top[:, first], gap2[:, first], REACH, exp2[:, first], ALU.max, ALU.add)
+        nc.vector.scalar_tensor_tensor(top[:, second], exp2[:, second], REACH, a0[:, second], ALU.max, ALU.add)
         for c in halves:
             nc.scalar.activation(logs[:, c], total[:, c], ACT.Ln)
-        for c, queue, op in zip(halves, (nc.sync, nc.scalar), (ALU.add, ALU.subtract)):
-            nc.vector.scalar_tensor_tensor(result[:, c], logs[:, c], REACH, top[:, c], ALU.subtract, op)
+        for c, queue in zip(halves, (nc.sync, nc.scalar)):
+            nc.vector.scalar_tensor_tensor(result[:, c], logs[:, c], REACH, top[:, c], ALU.subtract, ALU.add)
             queue.dma_start(out[:, c], result[:, c])

@@ -25,7 +25,6 @@ LIST_ROWS = 16
 PIECE = 128
 PIECES_ON_VECTOR = 2
 HALF = NODES // 2
-LAST_WIDTHS = (128, 64, 64)
 REACH = 40.0
 
 
@@ -112,53 +111,63 @@ def tile_picked_yspn_sum_p_kernel(
             else:
                 nc.scalar.copy(h[:, cols], acc[:])
 
-        left0, a0, left1, gap01, left2, short2, gap2 = (
-            node_tile(name) for name in ("left0", "a0", "left1", "gap01", "left2", "short2", "gap2")
+        halves = [slice(c, c + HALF) for c in range(0, NODES, HALF)]
+        first, second = halves
+        left0, left1, left2, a0, a1, a2, gap01, top01, gap2 = (
+            node_tile(name) for name in ("left0", "left1", "left2", "a0", "a1", "a2", "gap01", "top01", "gap2")
         )
         exp01 = held.tile([P, 2, NODES], F32, align_bytes=64)
-        term01 = held.tile([P, 2, NODES], F32, align_bytes=64, tag="term01")
+        term01 = held.tile([P, 2, NODES], F32, align_bytes=64)
         exp2, sum01, term2, total, top, logs, result = (
             node_tile(name) for name in ("exp2", "sum01", "term2", "total", "top", "logs", "result")
         )
-        halves = [slice(c, c + HALF) for c in range(0, NODES, HALF)]
 
-        def gather_and(dst, listed, other, op):
-            for c in halves:
-                nc.vector.tensor_tensor(dst[:, c], h[:].indirect(entries(listed, c)), other[:, c], op)
+        def fetch_on_scalar(dst, listed, c):
+            nc.scalar.activation(dst[:, c], h[:].indirect(entries(listed, c)), ACT.Copy)
 
-        first, second = halves
+        def fetch_on_vector(dst, listed, c):
+            nc.vector.tensor_copy(dst[:, c], h[:].indirect(entries(listed, c)))
 
-        def gather_half(dst, listed, other, op, c):
-            nc.vector.tensor_tensor(dst[:, c], h[:].indirect(entries(listed, c)), other[:, c], op)
+        def fetch_and_add(dst, listed, other, c):
+            nc.vector.tensor_tensor(dst[:, c], h[:].indirect(entries(listed, c)), other[:, c], ALU.add)
 
+        def plain(dst, x, y, op, c):
+            nc.vector.tensor_tensor(dst[:, c], x[:, c], y[:, c], op)
+
+        def exps01(c):
+            nc.scalar.activation(exp01[:, 0, c], gap01[:, c], ACT.Exp, scale=-1.0)
+            nc.scalar.activation(exp01[:, 1, c], gap01[:, c], ACT.Exp)
+
+        fetch_on_scalar(left1, p1, first)
+        fetch_on_vector(left0, p0, first)
+        fetch_on_scalar(left0, p0, second)
+        fetch_on_scalar(left1, p1, second)
+        fetch_on_scalar(left2, p2, first)
+        fetch_on_scalar(left2, p2, second)
+        fetch_and_add(a1, q1, left1, first)
+        fetch_and_add(a0, q0, left0, first)
+        fetch_and_add(a0, q0, left0, second)
+        plain(gap01, a1, a0, ALU.subtract, first)
+        fetch_and_add(a1, q1, left1, second)
+        plain(top01, a1, a0, ALU.max, first)
+        fetch_and_add(a2, q2, left2, first)
+        plain(gap01, a1, a0, ALU.subtract, second)
+        fetch_and_add(a2, q2, left2, second)
+        plain(top01, a1, a0, ALU.max, second)
+        plain(gap2, a2, top01, ALU.subtract, first)
+        plain(gap2, a2, top01, ALU.subtract, second)
         for c in halves:
-            nc.vector.tensor_copy(left0[:, c], h[:].indirect(entries(p0, c)))
-        gather_and(a0, q0, left0, ALU.add)
-        gather_and(left1, p1, a0, ALU.subtract)
-        nc.vector.tensor_tensor(left2[:], h[:].indirect(p2[:]), a0[:], ALU.subtract)
-        gaps01 = (gap01[:, first], left1[:, first])
-        gather_half(gap01, q1, left1, ALU.add, first)
-        gather_half(short2, q2, left2, ALU.add, second)
-        nc.vector.scalar_tensor_tensor(short2[:, first], gaps01[0], 0.0, left2[:, first], ALU.max, ALU.subtract)
-        nc.vector.tensor_tensor(gaps01[1], h[:].indirect(entries(q1, second)), left1[:, second], ALU.add)
-        gather_half(gap2, q2, short2, ALU.subtract, first)
-        nc.vector.scalar_tensor_tensor(gap2[:, second], gaps01[1], 0.0, short2[:, second], ALU.max, ALU.subtract)
-        for c, gap in zip(halves, gaps01):
-            nc.scalar.activation(exp01[:, 0, c], gap, ACT.Exp, scale=-1.0)
-            nc.scalar.activation(exp01[:, 1, c], gap, ACT.Exp)
-        nc.scalar.activation(exp2[:, first], gap2[:, first], ACT.Exp)
-        nc.scalar.activation(exp2[:, second], gap2[:, second], ACT.Exp, scale=-1.0)
+            exps01(c)
+        for c in halves:
+            nc.scalar.activation(exp2[:, c], gap2[:, c], ACT.Exp)
 
         for c in halves:
             nc.vector.scalar_tensor_tensor(term01[:, :, c], exp01[:, :, c], 1.0, mix[:, 0:2, c], ALU.min, ALU.mult)
         nc.vector.scalar_tensor_tensor(term2[:], exp2[:], math.exp(REACH), mix[:, 2, :], ALU.min, ALU.mult)
         nc.vector.tensor_tensor(sum01[:], term01[:, 0, :], term01[:, 1, :], ALU.add)
-        nc.vector.scalar_tensor_tensor(exp2[:, first], gaps01[0], 0.0, a0[:, first], ALU.max, ALU.add)
-        nc.vector.scalar_tensor_tensor(exp2[:, second], gaps01[1], REACH, short2[:, second], ALU.add, ALU.max)
+        nc.vector.scalar_tensor_tensor(top[:], gap2[:], REACH, top01[:], ALU.max, ALU.add)
         for c in halves:
-            nc.vector.tensor_tensor(total[:, c], sum01[:, c], term2[:, c], ALU.add)
-        nc.vector.scalar_tensor_tensor(top[:, first], gap2[:, first], REACH, exp2[:, first], ALU.max, ALU.add)
-        nc.vector.scalar_tensor_tensor(top[:, second], exp2[:, second], REACH, a0[:, second], ALU.max, ALU.add)
+            plain(total, sum01, term2, ALU.add, c)
         for c in halves:
             nc.scalar.activation(logs[:, c], total[:, c], ACT.Ln)
         for c, queue in zip(halves, (nc.sync, nc.scalar)):

@@ -25,7 +25,8 @@ LIST_ROWS = 16
 PIECE = 128
 PIECES_ON_VECTOR = 2
 HALF = NODES // 2
-REACH = 40.0
+REACH = 28.0
+SHIFT = 24
 
 
 def tile_picked_yspn_sum_p_kernel(
@@ -113,13 +114,13 @@ def tile_picked_yspn_sum_p_kernel(
 
         halves = [slice(c, c + HALF) for c in range(0, NODES, HALF)]
         first, second = halves
-        left0, left1, left2, a0, a1, a2, gap01, top01, gap2 = (
-            node_tile(name) for name in ("left0", "left1", "left2", "a0", "a1", "a2", "gap01", "top01", "gap2")
+        whole = slice(0, NODES)
+        left0, left1, left2, other1, other2, a0, a1, short2, gap1, base, gap2 = (
+            node_tile(name)
+            for name in ("left0", "left1", "left2", "other1", "other2", "a0", "a1", "short2", "gap1", "base", "gap2")
         )
-        exp01 = held.tile([P, 2, NODES], F32, align_bytes=64)
-        term01 = held.tile([P, 2, NODES], F32, align_bytes=64)
-        exp2, sum01, term2, total, top, logs, result = (
-            node_tile(name) for name in ("exp2", "sum01", "term2", "total", "top", "logs", "result")
+        exp1, exp2, term1, sum01, term2, total, top, logs, result = (
+            node_tile(name) for name in ("exp1", "exp2", "term1", "sum01", "term2", "total", "top", "logs", "result")
         )
 
         def fetch_on_scalar(dst, listed, c):
@@ -134,42 +135,46 @@ def tile_picked_yspn_sum_p_kernel(
         def plain(dst, x, y, op, c):
             nc.vector.tensor_tensor(dst[:, c], x[:, c], y[:, c], op)
 
-        def exps01(c):
-            nc.scalar.activation(exp01[:, 0, c], gap01[:, c], ACT.Exp, scale=-1.0)
-            nc.scalar.activation(exp01[:, 1, c], gap01[:, c], ACT.Exp)
+        def form_base(c):
+            nc.vector.scalar_tensor_tensor(base[:, c], a1[:, c], REACH, a0[:, c], ALU.subtract, ALU.max)
 
+        def exp(dst, src, c):
+            nc.scalar.activation(dst[:, c], src[:, c], ACT.Exp)
+
+        own, rest = slice(0, 192), slice(192, NODES)
         fetch_on_scalar(left1, p1, first)
-        fetch_on_vector(left0, p0, first)
-        fetch_on_scalar(left0, p0, second)
+        fetch_on_vector(left0, p0, own)
         fetch_on_scalar(left1, p1, second)
-        fetch_on_scalar(left2, p2, first)
-        fetch_on_scalar(left2, p2, second)
+        fetch_on_scalar(left0, p0, rest)
+        fetch_on_scalar(other1, q0, second)
+        fetch_on_scalar(left2, p2, whole)
+        fetch_on_scalar(other2, q2, whole)
         fetch_and_add(a1, q1, left1, first)
         fetch_and_add(a0, q0, left0, first)
-        fetch_and_add(a0, q0, left0, second)
-        plain(gap01, a1, a0, ALU.subtract, first)
         fetch_and_add(a1, q1, left1, second)
-        plain(top01, a1, a0, ALU.max, first)
-        fetch_and_add(a2, q2, left2, first)
-        plain(gap01, a1, a0, ALU.subtract, second)
-        fetch_and_add(a2, q2, left2, second)
-        plain(top01, a1, a0, ALU.max, second)
-        plain(gap2, a2, top01, ALU.subtract, first)
-        plain(gap2, a2, top01, ALU.subtract, second)
+        form_base(first)
+        plain(a0, other1, left0, ALU.add, second)
+        plain(gap1, a1, a0, ALU.subtract, first)
+        form_base(second)
+        plain(short2, left2, base, ALU.subtract, first)
+        plain(gap1, a1, a0, ALU.subtract, second)
+        plain(short2, left2, base, ALU.subtract, second)
         for c in halves:
-            exps01(c)
+            plain(gap2, short2, other2, ALU.add, c)
+        exp(exp1, gap1, whole)
         for c in halves:
-            nc.scalar.activation(exp2[:, c], gap2[:, c], ACT.Exp)
+            exp(exp2, gap2, c)
 
-        for c in halves:
-            nc.vector.scalar_tensor_tensor(term01[:, :, c], exp01[:, :, c], 1.0, mix[:, 0:2, c], ALU.min, ALU.mult)
-        nc.vector.scalar_tensor_tensor(term2[:], exp2[:], math.exp(REACH), mix[:, 2, :], ALU.min, ALU.mult)
-        nc.vector.tensor_tensor(sum01[:], term01[:, 0, :], term01[:, 1, :], ALU.add)
-        nc.vector.scalar_tensor_tensor(top[:], gap2[:], REACH, top01[:], ALU.max, ALU.add)
+        nc.vector.scalar_tensor_tensor(term1[:], exp1[:], math.exp(REACH), mix[:, 1, :], ALU.min, ALU.mult)
+        nc.vector.scalar_tensor_tensor(term2[:], exp2[:], math.exp(2 * REACH), mix[:, 2, :], ALU.min, ALU.mult)
+        nc.vector.tensor_tensor(sum01[:], term1[:], mix[:, 0, :], ALU.add)
+        nc.vector.scalar_tensor_tensor(top[:], gap2[:], 2 * REACH, base[:], ALU.max, ALU.add)
         for c in halves:
             plain(total, sum01, term2, ALU.add, c)
         for c in halves:
-            nc.scalar.activation(logs[:, c], total[:, c], ACT.Ln)
+            nc.scalar.activation(logs[:, c], total[:, c], ACT.Ln, scale=2.0**-SHIFT)
         for c, queue in zip(halves, (nc.sync, nc.scalar)):
-            nc.vector.scalar_tensor_tensor(result[:, c], logs[:, c], REACH, top[:, c], ALU.subtract, ALU.add)
+            nc.vector.scalar_tensor_tensor(
+                result[:, c], logs[:, c], SHIFT * math.log(2.0) - 2 * REACH, top[:, c], ALU.add, ALU.add
+            )
             queue.dma_start(out[:, c], result[:, c])

@@ -141,7 +141,7 @@ def tile_picked_yspn_sum_p_kernel(
         def exp(dst, src, c):
             nc.scalar.activation(dst[:, c], src[:, c], ACT.Exp)
 
-        own, rest = slice(0, 192), slice(192, NODES)
+        own, rest = slice(0, 160), slice(160, NODES)
         fetch_on_scalar(left1, p1, first)
         fetch_on_vector(left0, p0, own)
         fetch_on_scalar(left1, p1, second)

@@ -24,6 +24,8 @@ SCALE_ROWS = 4
 LIST_ROWS = 16
 PIECE = 128
 PIECES_ON_VECTOR = 2
+LATE = 64
+SPLIT = 64
 HALF = NODES // 2
 REACH = 28.0
 SHIFT = 24
@@ -61,7 +63,7 @@ def tile_picked_yspn_sum_p_kernel(
         word_table = held.tile([P, LEAVES], I32, align_bytes=64)
         nc.sync.dma_start(word_table[:], x_words[0].rearrange("p n t -> p (n t)").bitcast(I32))
 
-        w_raw = held.tile([P, PACK, ROWS], F32, align_bytes=64)
+        w_raw = held.tile([P, PACK, ROWS], F32, align_bytes=64, tag="staged")
         nc.sync.dma_start(w_raw[:], w1.rearrange("(p t) m -> p t m", t=PACK))
 
         p0 = load_list("p0", pos1)
@@ -76,8 +78,11 @@ def tile_picked_yspn_sum_p_kernel(
 
         w_grouped = held.tile([P, ROWS, PACK], BF16, align_bytes=64)
         nc.scalar.copy(
-            w_grouped[:].rearrange("p (c i) t -> p c t i", i=LINE),
-            w_raw[:].rearrange("p t (c i) -> p c t i", i=LINE),
+            w_grouped[:, :SPLIT, :].rearrange("p (c i) t -> p c t i", i=LINE),
+            w_raw[:, :, :SPLIT].rearrange("p t (c i) -> p c t i", i=LINE),
+        )
+        nc.gpsimd.tensor_scalar(
+            w_grouped[:, SPLIT:, :], w_raw[:, :, SPLIT:].rearrange("p t m -> p m t"), 1.0, 0.0, ALU.mult, ALU.add
         )
         w_codes = held.tile([P, ROWS], U32, align_bytes=64)
         w_scales = held.tile([P, ROWS], U8, align_bytes=64)
@@ -91,18 +96,24 @@ def tile_picked_yspn_sum_p_kernel(
             in_=w_grouped[:].rearrange("p m t -> p (m t)"),
         )
 
-        picked_words = held.tile([P, PICKED], I32, align_bytes=64)
-        nc.vector.tensor_copy(picked_words[:].bitcast(U32), word_table[:].bitcast(U32).indirect(idx[:]))
+        early = PICKED - LATE
+        early_words = held.tile([P, early], I32, align_bytes=64)
+        nc.vector.tensor_copy(early_words[:].bitcast(U32), word_table[:].bitcast(U32).indirect(entries(idx, slice(0, early))))
+        late_words = held.tile([P, LATE], I32, align_bytes=64, tag="staged")
+        nc.vector.tensor_copy(
+            late_words[:].bitcast(U32), word_table[:].bitcast(U32).indirect(entries(idx, slice(early, PICKED)))
+        )
 
         h = held.tile([P, PICKED], F32, align_bytes=64)
-        for piece in range(PICKED // PIECE):
-            cols = slice(piece * PIECE, (piece + 1) * PIECE)
-            acc = psum.tile([P, PIECE], F32, name="acc%d" % piece)
+        starts = [0, 128, 256, 384, early, PICKED]
+        for piece in range(len(starts) - 1):
+            cols = slice(starts[piece], starts[piece + 1])
+            acc = psum.tile([P, cols.stop - cols.start], F32, name="acc%d" % piece)
             nc.tensor.matmul_mx(
                 out=acc[:],
                 lhsT=w_codes[:].bitcast(FP8X4),
                 lhsT_scale=w_scales[:],
-                rhs=picked_words[:, cols].bitcast(FP8X4),
+                rhs=(early_words[:, cols] if cols.stop <= early else late_words[:]).bitcast(FP8X4),
                 rhs_scale=picked_scales[:, cols],
                 start=True,
                 stop=True,

@@ -158,23 +158,24 @@ def tile_picked_yspn_sum_p_kernel(
         fetch_on_scalar(left1, p1, second)
         fetch_on_scalar(left0, p0, rest)
         fetch_on_scalar(other1, q0, second)
-        fetch_on_scalar(left2, p2, whole)
-        fetch_on_scalar(other2, q2, whole)
+        fetch_on_scalar(left2, p2, second)
+        fetch_on_scalar(left2, p2, first)
+        fetch_on_scalar(other2, q2, first)
         fetch_and_add(a1, q1, left1, first)
         fetch_and_add(a0, q0, left0, first)
         fetch_and_add(a1, q1, left1, second)
         form_base(first)
         plain(a0, other1, left0, ALU.add, second)
         plain(gap1, a1, a0, ALU.subtract, first)
+        fetch_and_add(other2, q2, left2, second)
         form_base(second)
         plain(short2, left2, base, ALU.subtract, first)
         plain(gap1, a1, a0, ALU.subtract, second)
-        plain(short2, left2, base, ALU.subtract, second)
-        for c in halves:
-            plain(gap2, short2, other2, ALU.add, c)
+        plain(gap2, other2, base, ALU.subtract, second)
+        plain(gap2, short2, other2, ALU.add, first)
         exp(exp1, gap1, whole)
-        for c in halves:
-            exp(exp2, gap2, c)
+        exp(exp2, gap2, second)
+        exp(exp2, gap2, first)
 
         nc.vector.scalar_tensor_tensor(term1[:], exp1[:], math.exp(REACH), mix[:, 1, :], ALU.min, ALU.mult)
         nc.vector.scalar_tensor_tensor(term2[:], exp2[:], math.exp(2 * REACH), mix[:, 2, :], ALU.min, ALU.mult)

@@ -2,6 +2,7 @@ import math
 from contextlib import ExitStack
 
 import concourse.mybir as mybir
+from concourse.masks import make_identity
 
 K, LEAVES, PICKED, NODES, ROWS, TERMS = 512, 1024, 512, 256, 128, 3
 FLOPS = 2 * K * ROWS * PICKED
@@ -24,7 +25,7 @@ SCALE_ROWS = 4
 LIST_ROWS = 16
 PIECE = 128
 PIECES_ON_VECTOR = 2
-LATE = 64
+LATE = 128
 SPLIT = 64
 HALF = NODES // 2
 REACH = 28.0
@@ -76,6 +77,9 @@ def tile_picked_yspn_sum_p_kernel(
         mix = held.tile([P, TERMS, NODES], F32)
         nc.sync.dma_start(mix[:], mixw.rearrange("d p v -> p d v"))
 
+        identity = held.tile([P, P], F32, align_bytes=64)
+        make_identity(nc, identity[:])
+
         w_grouped = held.tile([P, ROWS, PACK], BF16, align_bytes=64)
         nc.scalar.copy(
             w_grouped[:, :SPLIT, :].rearrange("p (c i) t -> p c t i", i=LINE),
@@ -105,7 +109,7 @@ def tile_picked_yspn_sum_p_kernel(
         )
 
         h = held.tile([P, PICKED], F32, align_bytes=64)
-        starts = [0, 128, 256, 384, early, PICKED]
+        starts = [0, 128, 256, early, PICKED]
         for piece in range(len(starts) - 1):
             cols = slice(starts[piece], starts[piece + 1])
             acc = psum.tile([P, cols.stop - cols.start], F32, name="acc%d" % piece)
@@ -126,9 +130,9 @@ def tile_picked_yspn_sum_p_kernel(
         halves = [slice(c, c + HALF) for c in range(0, NODES, HALF)]
         first, second = halves
         whole = slice(0, NODES)
-        left0, left1, left2, other1, other2, a0, a1, short2, gap1, base, gap2 = (
+        left0, left1, left2, other1, other2, a0, a1, gap1, base, gap2 = (
             node_tile(name)
-            for name in ("left0", "left1", "left2", "other1", "other2", "a0", "a1", "short2", "gap1", "base", "gap2")
+            for name in ("left0", "left1", "left2", "other1", "other2", "a0", "a1", "gap1", "base", "gap2")
         )
         exp1, exp2, term1, sum01, term2, total, top, logs, result = (
             node_tile(name) for name in ("exp1", "exp2", "term1", "sum01", "term2", "total", "top", "logs", "result")
@@ -146,46 +150,69 @@ def tile_picked_yspn_sum_p_kernel(
         def plain(dst, x, y, op, c):
             nc.vector.tensor_tensor(dst[:, c], x[:, c], y[:, c], op)
 
-        def form_base(c):
-            nc.vector.scalar_tensor_tensor(base[:, c], a1[:, c], REACH, a0[:, c], ALU.subtract, ALU.max)
+        def form_base(dst, c):
+            nc.vector.scalar_tensor_tensor(dst[:, c], a1[:, c], REACH, a0[:, c], ALU.subtract, ALU.max)
 
         def exp(dst, src, c):
             nc.scalar.activation(dst[:, c], src[:, c], ACT.Exp)
 
-        own, rest = slice(0, 160), slice(160, NODES)
+        def fetch_negated(dst, listed, c):
+            nc.scalar.activation(dst[:, c], h[:].indirect(entries(listed, c)), ACT.Copy, scale=-1.0)
+
+        def turn_and_add(bank, tiles, c):
+            for i, tile in enumerate(tiles):
+                nc.tensor.matmul(
+                    bank[:], tile[:, c], identity[:], start=i == 0, stop=i == len(tiles) - 1, is_transpose=True
+                )
+
+        base_first = held.tile([P, HALF], F32, align_bytes=64)
         fetch_on_scalar(left1, p1, first)
-        fetch_on_vector(left0, p0, own)
+        fetch_on_vector(left0, p0, first)
+        fetch_on_vector(left0, p0, second)
         fetch_on_scalar(left1, p1, second)
-        fetch_on_scalar(left0, p0, rest)
         fetch_on_scalar(other1, q0, second)
         fetch_on_scalar(left2, p2, second)
-        fetch_on_scalar(left2, p2, first)
-        fetch_on_scalar(other2, q2, first)
+        fetch_negated(left2, p2, first)
+        fetch_negated(other2, q2, first)
         fetch_and_add(a1, q1, left1, first)
         fetch_and_add(a0, q0, left0, first)
         fetch_and_add(a1, q1, left1, second)
-        form_base(first)
         plain(a0, other1, left0, ALU.add, second)
+        form_base(base_first, first)
+        a2_second = held.tile([P, HALF], F32, align_bytes=64, tag="third")
+        nc.vector.tensor_tensor(a2_second[:], h[:].indirect(entries(q2, second)), left2[:, second], ALU.add)
+        form_base(base, second)
         plain(gap1, a1, a0, ALU.subtract, first)
-        fetch_and_add(other2, q2, left2, second)
-        form_base(second)
-        plain(short2, left2, base, ALU.subtract, first)
         plain(gap1, a1, a0, ALU.subtract, second)
-        plain(gap2, other2, base, ALU.subtract, second)
-        plain(gap2, short2, other2, ALU.add, first)
-        exp(exp1, gap1, whole)
+        nc.vector.tensor_tensor(gap2[:, second], a2_second[:], base[:, second], ALU.subtract)
+        turned = psum.tile([P, HALF], F32, name="turned")
+        turn_and_add(turned, (left2, base_first, other2), first)
+        exp(exp1, gap1, first)
+        exp_turned = held.tile([P, HALF], F32, align_bytes=64)
+        nc.scalar.activation(exp_turned[:], turned[:], ACT.Exp, scale=-1.0)
+        exp(exp1, gap1, second)
         exp(exp2, gap2, second)
-        exp(exp2, gap2, first)
+        back = psum.tile([P, HALF], F32, name="back")
+        nc.tensor.transpose(back[:], exp_turned[:], identity[:])
 
+        a2 = held.tile([P, HALF], F32, align_bytes=64, tag="third")
+        nc.vector.scalar_tensor_tensor(a2[:, first], left2[:, first], -1.0, other2[:, first], ALU.mult, ALU.subtract)
+        nc.vector.scalar_tensor_tensor(top[:, second], gap2[:, second], 2 * REACH, base[:, second], ALU.max, ALU.add)
         nc.vector.scalar_tensor_tensor(term1[:], exp1[:], math.exp(REACH), mix[:, 1, :], ALU.min, ALU.mult)
-        nc.vector.scalar_tensor_tensor(term2[:], exp2[:], math.exp(2 * REACH), mix[:, 2, :], ALU.min, ALU.mult)
+        nc.vector.scalar_tensor_tensor(
+            term2[:, second], exp2[:, second], math.exp(2 * REACH), mix[:, 2, second], ALU.min, ALU.mult
+        )
         nc.vector.tensor_tensor(sum01[:], term1[:], mix[:, 0, :], ALU.add)
-        nc.vector.scalar_tensor_tensor(top[:], gap2[:], 2 * REACH, base[:], ALU.max, ALU.add)
-        for c in halves:
+        nc.vector.scalar_tensor_tensor(
+            term2[:, first], back[:], math.exp(2 * REACH), mix[:, 2, first], ALU.min, ALU.mult
+        )
+        ending = (second, first)
+        for c in ending:
             plain(total, sum01, term2, ALU.add, c)
-        for c in halves:
+        nc.vector.scalar_tensor_tensor(top[:, first], base_first[:], 2 * REACH, a2[:, first], ALU.add, ALU.max)
+        for c in ending:
             nc.scalar.activation(logs[:, c], total[:, c], ACT.Ln, scale=2.0**-SHIFT)
-        for c, queue in zip(halves, (nc.sync, nc.scalar)):
+        for c, queue in zip(ending, (nc.sync, nc.scalar)):
             nc.vector.scalar_tensor_tensor(
                 result[:, c], logs[:, c], SHIFT * math.log(2.0) - 2 * REACH, top[:, c], ALU.add, ALU.add
             )

@@ -130,9 +130,9 @@ def tile_picked_yspn_sum_p_kernel(
         halves = [slice(c, c + HALF) for c in range(0, NODES, HALF)]
         first, second = halves
         whole = slice(0, NODES)
-        left0, left1, left2, other1, other2, a0, a1, gap1, base, gap2 = (
+        left0, left1, left2, other2, a0, a1, gap1, base = (
             node_tile(name)
-            for name in ("left0", "left1", "left2", "other1", "other2", "a0", "a1", "gap1", "base", "gap2")
+            for name in ("left0", "left1", "left2", "other2", "a0", "a1", "gap1", "base")
         )
         exp1, exp2, term1, sum01, term2, total, top, logs, result = (
             node_tile(name) for name in ("exp1", "exp2", "term1", "sum01", "term2", "total", "top", "logs", "result")
@@ -159,60 +159,52 @@ def tile_picked_yspn_sum_p_kernel(
         def fetch_negated(dst, listed, c):
             nc.scalar.activation(dst[:, c], h[:].indirect(entries(listed, c)), ACT.Copy, scale=-1.0)
 
-        def turn_and_add(bank, tiles, c):
-            for i, tile in enumerate(tiles):
-                nc.tensor.matmul(
-                    bank[:], tile[:, c], identity[:], start=i == 0, stop=i == len(tiles) - 1, is_transpose=True
-                )
+        def turn_and_add(i, tile, start=False, stop=False):
+            nc.tensor.matmul(turned[i][:], tile[:, halves[i]], identity[:], start=start, stop=stop, is_transpose=True)
 
-        base_first = held.tile([P, HALF], F32, align_bytes=64)
+        rest, own = slice(0, 64), slice(64, NODES)
         fetch_on_scalar(left1, p1, first)
-        fetch_on_vector(left0, p0, first)
-        fetch_on_vector(left0, p0, second)
+        fetch_on_vector(left0, p0, own)
+        fetch_on_scalar(left0, p0, rest)
         fetch_on_scalar(left1, p1, second)
-        fetch_on_scalar(other1, q0, second)
-        fetch_on_scalar(left2, p2, second)
-        fetch_negated(left2, p2, first)
-        fetch_negated(other2, q2, first)
+        for c in halves:
+            fetch_negated(left2, p2, c)
+            fetch_negated(other2, q2, c)
         fetch_and_add(a1, q1, left1, first)
-        fetch_and_add(a0, q0, left0, first)
+        fetch_and_add(a0, q0, left0, whole)
         fetch_and_add(a1, q1, left1, second)
-        plain(a0, other1, left0, ALU.add, second)
-        form_base(base_first, first)
-        a2_second = held.tile([P, HALF], F32, align_bytes=64, tag="third")
-        nc.vector.tensor_tensor(a2_second[:], h[:].indirect(entries(q2, second)), left2[:, second], ALU.add)
-        form_base(base, second)
+        form_base(base, first)
         plain(gap1, a1, a0, ALU.subtract, first)
+        form_base(base, second)
         plain(gap1, a1, a0, ALU.subtract, second)
-        nc.vector.tensor_tensor(gap2[:, second], a2_second[:], base[:, second], ALU.subtract)
-        turned = psum.tile([P, HALF], F32, name="turned")
-        turn_and_add(turned, (left2, base_first, other2), first)
-        exp(exp1, gap1, first)
-        exp_turned = held.tile([P, HALF], F32, align_bytes=64)
-        nc.scalar.activation(exp_turned[:], turned[:], ACT.Exp, scale=-1.0)
-        exp(exp1, gap1, second)
-        exp(exp2, gap2, second)
-        back = psum.tile([P, HALF], F32, name="back")
-        nc.tensor.transpose(back[:], exp_turned[:], identity[:])
+        backs = []
+        turned = [psum.tile([P, HALF], F32, name="turned%d" % i) for i in range(len(halves))]
+        turn_and_add(0, left2, start=True)
+        turn_and_add(0, other2)
+        turn_and_add(1, left2, start=True)
+        turn_and_add(0, base, stop=True)
+        turn_and_add(1, base)
+        turn_and_add(1, other2, stop=True)
+        for i, c in enumerate(halves):
+            exp(exp1, gap1, c)
+            nc.scalar.activation(exp2[:, c], turned[i][:], ACT.Exp, scale=-1.0)
+        for i, c in enumerate(halves):
+            back = psum.tile([P, HALF], F32, name="back%d" % i)
+            nc.tensor.transpose(back[:], exp2[:, c], identity[:])
+            backs.append(back)
 
-        a2 = held.tile([P, HALF], F32, align_bytes=64, tag="third")
-        nc.vector.scalar_tensor_tensor(a2[:, first], left2[:, first], -1.0, other2[:, first], ALU.mult, ALU.subtract)
-        nc.vector.scalar_tensor_tensor(top[:, second], gap2[:, second], 2 * REACH, base[:, second], ALU.max, ALU.add)
+        a2 = node_tile("a2", "a0")
+        nc.vector.scalar_tensor_tensor(a2[:], left2[:], -1.0, other2[:], ALU.mult, ALU.subtract)
         nc.vector.scalar_tensor_tensor(term1[:], exp1[:], math.exp(REACH), mix[:, 1, :], ALU.min, ALU.mult)
-        nc.vector.scalar_tensor_tensor(
-            term2[:, second], exp2[:, second], math.exp(2 * REACH), mix[:, 2, second], ALU.min, ALU.mult
-        )
+        nc.vector.scalar_tensor_tensor(top[:], base[:], 2 * REACH, a2[:], ALU.add, ALU.max)
         nc.vector.tensor_tensor(sum01[:], term1[:], mix[:, 0, :], ALU.add)
-        nc.vector.scalar_tensor_tensor(
-            term2[:, first], back[:], math.exp(2 * REACH), mix[:, 2, first], ALU.min, ALU.mult
-        )
-        ending = (second, first)
-        for c in ending:
+        for back, c in zip(backs, halves):
+            nc.vector.scalar_tensor_tensor(term2[:, c], back[:], math.exp(2 * REACH), mix[:, 2, c], ALU.min, ALU.mult)
+        for c in halves:
             plain(total, sum01, term2, ALU.add, c)
-        nc.vector.scalar_tensor_tensor(top[:, first], base_first[:], 2 * REACH, a2[:, first], ALU.add, ALU.max)
-        for c in ending:
+        for c in halves:
             nc.scalar.activation(logs[:, c], total[:, c], ACT.Ln, scale=2.0**-SHIFT)
-        for c, queue in zip(ending, (nc.sync, nc.scalar)):
+        for c, queue in zip(halves, (nc.sync, nc.scalar)):
             nc.vector.scalar_tensor_tensor(
                 result[:, c], logs[:, c], SHIFT * math.log(2.0) - 2 * REACH, top[:, c], ALU.add, ALU.add
             )

import math
from contextlib import ExitStack

import concourse.mybir as mybir
from concourse.masks import make_identity

K, LEAVES, PICKED, NODES, ROWS, TERMS = 512, 1024, 512, 256, 128, 3
FLOPS = 2 * K * ROWS * PICKED

F32 = mybir.dt.float32
BF16 = mybir.dt.bfloat16
I32 = mybir.dt.int32
U32 = mybir.dt.uint32
U16 = mybir.dt.uint16
U8 = mybir.dt.uint8
FP8X4 = mybir.dt.float8_e4m3fn_x4
ALU = mybir.AluOpType
ACT = mybir.ActivationFunctionType

P = 128
PACK = 4
LINE = 4
QUADRANT = 32
SCALE_ROWS = 4
LIST_ROWS = 16
PIECE = 128
PIECES_ON_VECTOR = 2
LATE = 128
SPLIT = 64
HALF = NODES // 2
REACH = 28.0
SHIFT = 24


def tile_picked_yspn_sum_p_kernel(
    tc, x_words, x_scales, w1, mixw, offs, pos1, pos2, pos3, right1, right2, right3, out
):
    nc = tc.nc
    with ExitStack() as ctx:
        held = ctx.enter_context(tc.tile_pool(name="held", bufs=1))
        psum = ctx.enter_context(tc.psum_pool(name="psum", bufs=1))

        def load_list(name, src):
            tile = held.tile(list(src.shape), U16, name=name)
            nc.sync.dma_start(tile[:], src)
            return tile

        def entries(tile, cols):
            return tile[:, cols.start // LIST_ROWS : cols.stop // LIST_ROWS]

        def node_tile(name, bytes_of=None):
            return held.tile([P, NODES], F32, align_bytes=64, name=name, tag=bytes_of or name)

        idx = load_list("idx", offs)

        scale_table = held.tile([P, LEAVES], U8, align_bytes=64)
        for quad, queue in enumerate((nc.sync, nc.sync, nc.scalar, nc.scalar)):
            rows = x_scales[0][SCALE_ROWS * quad : SCALE_ROWS * (quad + 1), :].bitcast(I32)
            queue.dma_start(
                scale_table[QUADRANT * quad : QUADRANT * (quad + 1), :].bitcast(I32),
                rows.unsqueeze(0).to_broadcast([QUADRANT // SCALE_ROWS, SCALE_ROWS, rows.shape[1]]),
            )

        word_table = held.tile([P, LEAVES], I32, align_bytes=64)
        nc.sync.dma_start(word_table[:], x_words[0].rearrange("p n t -> p (n t)").bitcast(I32))

        w_raw = held.tile([P, PACK, ROWS], F32, align_bytes=64, tag="staged")
        nc.sync.dma_start(w_raw[:], w1.rearrange("(p t) m -> p t m", t=PACK))

        p0 = load_list("p0", pos1)
        q0 = load_list("q0", right1)
        p1 = load_list("p1", pos2)
        q1 = load_list("q1", right2)
        p2 = load_list("p2", pos3)
        q2 = load_list("q2", right3)

        mix = held.tile([P, TERMS, NODES], F32)
        nc.sync.dma_start(mix[:], mixw.rearrange("d p v -> p d v"))

        identity = held.tile([P, P], F32, align_bytes=64)
        make_identity(nc, identity[:])

        w_grouped = held.tile([P, ROWS, PACK], BF16, align_bytes=64)
        nc.scalar.copy(
            w_grouped[:, :SPLIT, :].rearrange("p (c i) t -> p c t i", i=LINE),
            w_raw[:, :, :SPLIT].rearrange("p t (c i) -> p c t i", i=LINE),
        )
        nc.gpsimd.tensor_scalar(
            w_grouped[:, SPLIT:, :], w_raw[:, :, SPLIT:].rearrange("p t m -> p m t"), 1.0, 0.0, ALU.mult, ALU.add
        )
        w_codes = held.tile([P, ROWS], U32, align_bytes=64)
        w_scales = held.tile([P, ROWS], U8, align_bytes=64)

        picked_scales = held.tile([P, PICKED], U8, align_bytes=64)
        nc.vector.tensor_copy(picked_scales[:], scale_table[:].indirect(idx[:]))

        nc.vector.quantize_mx(
            out=w_codes[:].bitcast(FP8X4),
            scales=w_scales[:],
            in_=w_grouped[:].rearrange("p m t -> p (m t)"),
        )

        early = PICKED - LATE
        early_words = held.tile([P, early], I32, align_bytes=64)
        nc.vector.tensor_copy(early_words[:].bitcast(U32), word_table[:].bitcast(U32).indirect(entries(idx, slice(0, early))))
        late_words = held.tile([P, LATE], I32, align_bytes=64, tag="staged")
        nc.vector.tensor_copy(
            late_words[:].bitcast(U32), word_table[:].bitcast(U32).indirect(entries(idx, slice(early, PICKED)))
        )

        h = held.tile([P, PICKED], F32, align_bytes=64)
        starts = [0, 128, 256, early, PICKED]
        for piece in range(len(starts) - 1):
            cols = slice(starts[piece], starts[piece + 1])
            acc = psum.tile([P, cols.stop - cols.start], F32, name="acc%d" % piece)
            nc.tensor.matmul_mx(
                out=acc[:],
                lhsT=w_codes[:].bitcast(FP8X4),
                lhsT_scale=w_scales[:],
                rhs=(early_words[:, cols] if cols.stop <= early else late_words[:]).bitcast(FP8X4),
                rhs_scale=picked_scales[:, cols],
                start=True,
                stop=True,
            )
            if piece < PIECES_ON_VECTOR:
                nc.vector.tensor_copy(h[:, cols], acc[:])
            else:
                nc.scalar.copy(h[:, cols], acc[:])

        halves = [slice(c, c + HALF) for c in range(0, NODES, HALF)]
        first, second = halves
        whole = slice(0, NODES)
        left0, left1, left2, other2, a0, a1, gap1, base = (
            node_tile(name)
            for name in ("left0", "left1", "left2", "other2", "a0", "a1", "gap1", "base")
        )
        exp1, exp2, term1, sum01, term2, total, top, logs, result = (
            node_tile(name) for name in ("exp1", "exp2", "term1", "sum01", "term2", "total", "top", "logs", "result")
        )

        def fetch_on_scalar(dst, listed, c):
            nc.scalar.activation(dst[:, c], h[:].indirect(entries(listed, c)), ACT.Copy)

        def fetch_on_vector(dst, listed, c):
            nc.vector.tensor_copy(dst[:, c], h[:].indirect(entries(listed, c)))

        def fetch_and_add(dst, listed, other, c):
            nc.vector.tensor_tensor(dst[:, c], h[:].indirect(entries(listed, c)), other[:, c], ALU.add)

        def plain(dst, x, y, op, c):
            nc.vector.tensor_tensor(dst[:, c], x[:, c], y[:, c], op)

        def form_base(dst, c):
            nc.vector.scalar_tensor_tensor(dst[:, c], a1[:, c], REACH, a0[:, c], ALU.subtract, ALU.max)

        def exp(dst, src, c):
            nc.scalar.activation(dst[:, c], src[:, c], ACT.Exp)

        def fetch_negated(dst, listed, c):
            nc.scalar.activation(dst[:, c], h[:].indirect(entries(listed, c)), ACT.Copy, scale=-1.0)

        def turn_and_add(i, tile, start=False, stop=False):
            nc.tensor.matmul(turned[i][:], tile[:, halves[i]], identity[:], start=start, stop=stop, is_transpose=True)

        rest, own = slice(0, 64), slice(64, NODES)
        fetch_on_scalar(left1, p1, first)
        fetch_on_vector(left0, p0, own)
        fetch_on_scalar(left0, p0, rest)
        fetch_on_scalar(left1, p1, second)
        for c in halves:
            fetch_negated(left2, p2, c)
            fetch_negated(other2, q2, c)
        fetch_and_add(a1, q1, left1, first)
        fetch_and_add(a0, q0, left0, whole)
        fetch_and_add(a1, q1, left1, second)
        form_base(base, first)
        plain(gap1, a1, a0, ALU.subtract, first)
        form_base(base, second)
        plain(gap1, a1, a0, ALU.subtract, second)
        backs = []
        turned = [psum.tile([P, HALF], F32, name="turned%d" % i) for i in range(len(halves))]
        turn_and_add(0, left2, start=True)
        turn_and_add(0, other2)
        turn_and_add(1, left2, start=True)
        turn_and_add(0, base, stop=True)
        turn_and_add(1, base)
        turn_and_add(1, other2, stop=True)
        for i, c in enumerate(halves):
            exp(exp1, gap1, c)
            nc.scalar.activation(exp2[:, c], turned[i][:], ACT.Exp, scale=-1.0)
        for i, c in enumerate(halves):
            back = psum.tile([P, HALF], F32, name="back%d" % i)
            nc.tensor.transpose(back[:], exp2[:, c], identity[:])
            backs.append(back)

        a2 = node_tile("a2", "a0")
        nc.vector.scalar_tensor_tensor(a2[:], left2[:], -1.0, other2[:], ALU.mult, ALU.subtract)
        nc.vector.scalar_tensor_tensor(term1[:], exp1[:], math.exp(REACH), mix[:, 1, :], ALU.min, ALU.mult)
        nc.vector.scalar_tensor_tensor(top[:], base[:], 2 * REACH, a2[:], ALU.add, ALU.max)
        nc.vector.tensor_tensor(sum01[:], term1[:], mix[:, 0, :], ALU.add)
        for back, c in zip(backs, halves):
            nc.vector.scalar_tensor_tensor(term2[:, c], back[:], math.exp(2 * REACH), mix[:, 2, c], ALU.min, ALU.mult)
        for c in halves:
            plain(total, sum01, term2, ALU.add, c)
        for c in halves:
            nc.scalar.activation(logs[:, c], total[:, c], ACT.Ln, scale=2.0**-SHIFT)
        for c, queue in zip(halves, (nc.sync, nc.scalar)):
            nc.vector.scalar_tensor_tensor(
                result[:, c], logs[:, c], SHIFT * math.log(2.0) - 2 * REACH, top[:, c], ALU.add, ALU.add
            )
            queue.dma_start(out[:, c], result[:, c])
